import numpy as np
import ml_dtypes

BF16 = ml_dtypes.bfloat16


def bf(x):
    return np.asarray(x, np.float32).astype(BF16)


def f32(x):
    return np.asarray(x, np.float32)


def f64(x):
    return np.asarray(x).astype(np.float64)


def striped(idx):
    return np.tile(idx.reshape(-1, 16).T, (8, 1))


S, K, M, N = 256, 128, 128, 64


def setup_inputs():
    return {"base": bf(np.random.standard_normal((M, S))), "x": bf(np.random.standard_normal((K, N))), "w": bf(np.random.standard_normal((K, M)) / np.sqrt(K)), "s": f32(0.5 + np.random.random_sample((M, 1))), "b": f32(0.5 * np.random.standard_normal((M, 1))), "offs": striped(np.random.permutation(S)[:N])}


def reference(base, x, w, s, b, offs):
    idx = offs[:16].T.reshape(-1)
    z = f64(base).copy()
    z[:, idx] = f64(w).T @ f64(x)
    return z * f64(s) + f64(b)

@@ -1,0 +1,44 @@
+import concourse.mybir as mybir
+from concourse.masks import make_identity
+
+BF16, F32, U16 = mybir.dt.bfloat16, mybir.dt.float32, mybir.dt.uint16
+MULT, ADD = mybir.AluOpType.mult, mybir.AluOpType.add
+
+P = 128
+TOKENS = 256
+PICKED = 64
+
+FLOPS = 2 * P * P * PICKED
+
+
+def tile_scatter_matmul_kernel(tc, base, x, w, s, b, offs, out):
+    nc = tc.nc
+    with (
+        tc.tile_pool(name="held", bufs=1) as held,
+        tc.psum_pool(name="psum", bufs=1) as psum,
+    ):
+        offsets = held.tile([P, PICKED // 16], U16, name="offsets")
+        nc.sync.dma_start(offsets[:], offs)
+
+        base_tile = held.tile([P, TOKENS], BF16, name="base_tile")
+        nc.scalar.dma_start(base_tile[:], base)
+        weights = held.tile([P, P], BF16, name="weights")
+        nc.sync.dma_start(weights[:], w)
+        moving = held.tile([P, PICKED], BF16, name="moving")
+        nc.scalar.dma_start(moving[:], x)
+        gain = held.tile([P, 1], F32, name="gain")
+        nc.sync.dma_start(gain[:], s)
+        shift = held.tile([P, 1], F32, name="shift")
+        nc.scalar.dma_start(shift[:], b)
+
+        ident = held.tile([P, P], BF16, name="ident")
+        make_identity(nc, ident[:])
+
+        window = psum.tile([P, TOKENS], F32, name="window")
+        nc.tensor.matmul(window[:], ident[:], base_tile[:], start=True, stop=True)
+
+        nc.tensor.matmul(window[:].indirect(offsets[:]), weights[:], moving[:], start=True, stop=True)
+
+        result = held.tile([P, TOKENS], F32, name="result")
+        nc.vector.tensor_scalar(result[:], window[:], gain[:], shift[:], MULT, ADD)
+        nc.sync.dma_start(out, result[:])

@@ -7,6 +7,7 @@ MULT, ADD = mybir.AluOpType.mult, mybir.AluOpType.add
 P = 128
 TOKENS = 256
 PICKED = 64
+HALF = TOKENS // 2
 
 FLOPS = 2 * P * P * PICKED
 
@@ -40,5 +41,6 @@ def tile_scatter_matmul_kernel(tc, base, x, w, s, b, offs, out):
         nc.tensor.matmul(window[:].indirect(offsets[:]), weights[:], moving[:], start=True, stop=True)
 
         result = held.tile([P, TOKENS], F32, name="result")
-        nc.vector.tensor_scalar(result[:], window[:], gain[:], shift[:], MULT, ADD)
-        nc.sync.dma_start(out, result[:])
+        for queue, cols in ((nc.sync, slice(0, HALF)), (nc.scalar, slice(HALF, TOKENS))):
+            nc.vector.tensor_scalar(result[:, cols], window[:, cols], gain[:], shift[:], MULT, ADD)
+            queue.dma_start(out[:, cols], result[:, cols])

@@ -7,7 +7,6 @@ MULT, ADD = mybir.AluOpType.mult, mybir.AluOpType.add
 P = 128
 TOKENS = 256
 PICKED = 64
-HALF = TOKENS // 2
 
 FLOPS = 2 * P * P * PICKED
 
@@ -33,7 +32,8 @@ def tile_scatter_matmul_kernel(tc, base, x, w, s, b, offs, out):
         nc.scalar.dma_start(shift[:], b)
 
         ident = held.tile([P, P], BF16, name="ident")
-        make_identity(nc, ident[:])
+        nc.vector.memset(ident[:], 0.0)
+        make_identity(nc, ident[:], nomemset=True)
 
         window = psum.tile([P, TOKENS], F32, name="window")
         nc.tensor.matmul(window[:], ident[:], base_tile[:], start=True, stop=True)
@@ -41,6 +41,5 @@ def tile_scatter_matmul_kernel(tc, base, x, w, s, b, offs, out):
         nc.tensor.matmul(window[:].indirect(offsets[:]), weights[:], moving[:], start=True, stop=True)
 
         result = held.tile([P, TOKENS], F32, name="result")
-        for queue, cols in ((nc.sync, slice(0, HALF)), (nc.scalar, slice(HALF, TOKENS))):
-            nc.vector.tensor_scalar(result[:, cols], window[:, cols], gain[:], shift[:], MULT, ADD)
-            queue.dma_start(out[:, cols], result[:, cols])
+        nc.vector.tensor_scalar(result[:], window[:], gain[:], shift[:], MULT, ADD)
+        nc.sync.dma_start(out, result[:])

@@ -17,23 +17,27 @@ def tile_scatter_matmul_kernel(tc, base, x, w, s, b, offs, out):
         tc.tile_pool(name="held", bufs=1) as held,
         tc.psum_pool(name="psum", bufs=1) as psum,
     ):
+        rows = held.tile([2, P], F32, name="rows")
+        nc.sync.dma_start(rows[0:1, :], s.rearrange("m o -> o m"))
+        nc.scalar.dma_start(rows[1:2, :], b.rearrange("m o -> o m"))
+
         offsets = held.tile([P, PICKED // 16], U16, name="offsets")
         nc.sync.dma_start(offsets[:], offs)
-
         base_tile = held.tile([P, TOKENS], BF16, name="base_tile")
         nc.scalar.dma_start(base_tile[:], base)
         weights = held.tile([P, P], BF16, name="weights")
         nc.sync.dma_start(weights[:], w)
         moving = held.tile([P, PICKED], BF16, name="moving")
         nc.scalar.dma_start(moving[:], x)
-        gain = held.tile([P, 1], F32, name="gain")
-        nc.sync.dma_start(gain[:], s)
-        shift = held.tile([P, 1], F32, name="shift")
-        nc.scalar.dma_start(shift[:], b)
 
         ident = held.tile([P, P], BF16, name="ident")
         nc.vector.memset(ident[:], 0.0)
         make_identity(nc, ident[:], nomemset=True)
+        pair = held.tile([2, 2], F32, name="pair")
+        make_identity(nc, pair[:])
+
+        affine = psum.tile([P, 2], F32, name="affine")
+        nc.tensor.matmul(affine[:], rows[:], pair[:], start=True, stop=True)
 
         window = psum.tile([P, TOKENS], F32, name="window")
         nc.tensor.matmul(window[:], ident[:], base_tile[:], start=True, stop=True)
@@ -41,5 +45,5 @@ def tile_scatter_matmul_kernel(tc, base, x, w, s, b, offs, out):
         nc.tensor.matmul(window[:].indirect(offsets[:]), weights[:], moving[:], start=True, stop=True)
 
         result = held.tile([P, TOKENS], F32, name="result")
-        nc.vector.tensor_scalar(result[:], window[:], gain[:], shift[:], MULT, ADD)
+        nc.vector.tensor_scalar(result[:], window[:], affine[:, 0:1], affine[:, 1:2], MULT, ADD)
         nc.sync.dma_start(out, result[:])

@@ -7,6 +7,7 @@ MULT, ADD = mybir.AluOpType.mult, mybir.AluOpType.add
 P = 128
 TOKENS = 256
 PICKED = 64
+SQUARE = 32
 
 FLOPS = 2 * P * P * PICKED
 
@@ -17,9 +18,8 @@ def tile_scatter_matmul_kernel(tc, base, x, w, s, b, offs, out):
         tc.tile_pool(name="held", bufs=1) as held,
         tc.psum_pool(name="psum", bufs=1) as psum,
     ):
-        rows = held.tile([2, P], F32, name="rows")
-        nc.sync.dma_start(rows[0:1, :], s.rearrange("m o -> o m"))
-        nc.scalar.dma_start(rows[1:2, :], b.rearrange("m o -> o m"))
+        lying = held.tile([P, SQUARE], F32, name="lying", align_bytes=64)
+        nc.vector.memset(lying[:], 0.0)
 
         offsets = held.tile([P, PICKED // 16], U16, name="offsets")
         nc.sync.dma_start(offsets[:], offs)
@@ -29,21 +29,21 @@ def tile_scatter_matmul_kernel(tc, base, x, w, s, b, offs, out):
         nc.sync.dma_start(weights[:], w)
         moving = held.tile([P, PICKED], BF16, name="moving")
         nc.scalar.dma_start(moving[:], x)
+        nc.sync.dma_start(lying[0:P:SQUARE, :], s.rearrange("(q j) o -> q (j o)", j=SQUARE))
+        nc.scalar.dma_start(lying[1:P:SQUARE, :], b.rearrange("(q j) o -> q (j o)", j=SQUARE))
 
         ident = held.tile([P, P], BF16, name="ident")
         nc.vector.memset(ident[:], 0.0)
         make_identity(nc, ident[:], nomemset=True)
-        pair = held.tile([2, 2], F32, name="pair")
-        make_identity(nc, pair[:])
-
-        affine = psum.tile([P, 2], F32, name="affine")
-        nc.tensor.matmul(affine[:], rows[:], pair[:], start=True, stop=True)
 
         window = psum.tile([P, TOKENS], F32, name="window")
         nc.tensor.matmul(window[:], ident[:], base_tile[:], start=True, stop=True)
 
         nc.tensor.matmul(window[:].indirect(offsets[:]), weights[:], moving[:], start=True, stop=True)
 
+        upright = held.tile([P, SQUARE], F32, name="upright", align_bytes=64)
+        nc.vector.transpose(upright[:], lying[:])
+
         result = held.tile([P, TOKENS], F32, name="result")
-        nc.vector.tensor_scalar(result[:], window[:], affine[:, 0:1], affine[:, 1:2], MULT, ADD)
+        nc.vector.tensor_scalar(result[:], window[:], upright[:, 0:1], upright[:, 1:2], MULT, ADD)
         nc.sync.dma_start(out, result[:])

@@ -7,6 +7,7 @@ MULT, ADD = mybir.AluOpType.mult, mybir.AluOpType.add
 P = 128
 TOKENS = 256
 PICKED = 64
+HALF = P // 2
 SQUARE = 32
 
 FLOPS = 2 * P * P * PICKED
@@ -21,16 +22,17 @@ def tile_scatter_matmul_kernel(tc, base, x, w, s, b, offs, out):
         lying = held.tile([P, SQUARE], F32, name="lying", align_bytes=64)
         nc.vector.memset(lying[:], 0.0)
 
+        base_tile = held.tile([P, TOKENS], BF16, name="base_tile")
+        nc.sync.dma_start(base_tile[0:HALF, :], base[0:HALF, :])
+        nc.scalar.dma_start(base_tile[HALF:P, :], base[HALF:P, :])
         offsets = held.tile([P, PICKED // 16], U16, name="offsets")
         nc.sync.dma_start(offsets[:], offs)
-        base_tile = held.tile([P, TOKENS], BF16, name="base_tile")
-        nc.scalar.dma_start(base_tile[:], base)
         weights = held.tile([P, P], BF16, name="weights")
-        nc.sync.dma_start(weights[:], w)
+        nc.scalar.dma_start(weights[:], w)
         moving = held.tile([P, PICKED], BF16, name="moving")
-        nc.scalar.dma_start(moving[:], x)
-        nc.sync.dma_start(lying[0:P:SQUARE, :], s.rearrange("(q j) o -> q (j o)", j=SQUARE))
+        nc.sync.dma_start(moving[:], x)
         nc.scalar.dma_start(lying[1:P:SQUARE, :], b.rearrange("(q j) o -> q (j o)", j=SQUARE))
+        nc.sync.dma_start(lying[0:P:SQUARE, :], s.rearrange("(q j) o -> q (j o)", j=SQUARE))
 
         ident = held.tile([P, P], BF16, name="ident")
         nc.vector.memset(ident[:], 0.0)

import concourse.mybir as mybir
from concourse.masks import make_identity

BF16, F32, U16 = mybir.dt.bfloat16, mybir.dt.float32, mybir.dt.uint16
MULT, ADD = mybir.AluOpType.mult, mybir.AluOpType.add

P = 128
TOKENS = 256
PICKED = 64
HALF = P // 2
SQUARE = 32

FLOPS = 2 * P * P * PICKED


def tile_scatter_matmul_kernel(tc, base, x, w, s, b, offs, out):
    nc = tc.nc
    with (
        tc.tile_pool(name="held", bufs=1) as held,
        tc.psum_pool(name="psum", bufs=1) as psum,
    ):
        lying = held.tile([P, SQUARE], F32, name="lying", align_bytes=64)
        nc.vector.memset(lying[:], 0.0)

        base_tile = held.tile([P, TOKENS], BF16, name="base_tile")
        nc.sync.dma_start(base_tile[0:HALF, :], base[0:HALF, :])
        nc.scalar.dma_start(base_tile[HALF:P, :], base[HALF:P, :])
        offsets = held.tile([P, PICKED // 16], U16, name="offsets")
        nc.sync.dma_start(offsets[:], offs)
        weights = held.tile([P, P], BF16, name="weights")
        nc.scalar.dma_start(weights[:], w)
        moving = held.tile([P, PICKED], BF16, name="moving")
        nc.sync.dma_start(moving[:], x)
        nc.scalar.dma_start(lying[1:P:SQUARE, :], b.rearrange("(q j) o -> q (j o)", j=SQUARE))
        nc.sync.dma_start(lying[0:P:SQUARE, :], s.rearrange("(q j) o -> q (j o)", j=SQUARE))

        ident = held.tile([P, P], BF16, name="ident")
        nc.vector.memset(ident[:], 0.0)
        make_identity(nc, ident[:], nomemset=True)

        window = psum.tile([P, TOKENS], F32, name="window")
        nc.tensor.matmul(window[:], ident[:], base_tile[:], start=True, stop=True)

        nc.tensor.matmul(window[:].indirect(offsets[:]), weights[:], moving[:], start=True, stop=True)

        upright = held.tile([P, SQUARE], F32, name="upright", align_bytes=64)
        nc.vector.transpose(upright[:], lying[:])

        result = held.tile([P, TOKENS], F32, name="result")
        nc.vector.tensor_scalar(result[:], window[:], upright[:, 0:1], upright[:, 1:2], MULT, ADD)
        nc.sync.dma_start(out, result[:])
